import numpy as np
import ml_dtypes


def mxq(x, axis, fmt="e4m3"):
    dtype, down = {"e4m3": (ml_dtypes.float8_e4m3fn, 7), "e5m2": (ml_dtypes.float8_e5m2, 14)}[fmt]
    v = np.moveaxis(np.asarray(x, np.float32).astype(ml_dtypes.bfloat16).astype(np.float64), axis, -1)
    blocks = v.reshape(v.shape[:-1] + (-1, 32))
    amax = np.abs(blocks).max(-1, keepdims=True)
    byte = np.maximum(np.where(amax > 0, np.frexp(amax)[1] - 1 + 127, 0) - down, 1)
    scale = np.exp2(byte - 127.0)
    codes = (blocks / scale).astype(np.float32).astype(dtype).astype(np.float64)
    return np.moveaxis((codes * scale).reshape(v.shape), -1, axis)


WIDE = False


def mx_kscale(k):
    if not WIDE:
        return np.ones(k)
    levels = np.array([10, -10, 5, -5, 0])
    if k % 512:
        return np.exp2(np.random.permutation(np.resize(levels, k // 32))).repeat(32)
    a = np.empty((k // 512, 16))
    for p in range(k // 512):
        a[p, :8] = np.random.permutation(np.resize(levels, 8))
        for g in range(8):
            far = levels[np.abs(levels - a[p, g]) >= 10]
            a[p, g + 8] = far[np.random.randint(len(far))]
    return np.exp2(a.ravel()).repeat(32)


def f64(x):
    return np.asarray(x).astype(np.float64)


def striped(idx):
    return np.tile(np.asarray(idx).reshape(-1, 16).T, (8, 1)).astype(np.uint16)


def unstriped(offs):
    return offs[:16].T.reshape(-1).astype(np.int64)


E2M1 = np.array([0.0, 0.5, 1.0, 1.5, 2.0, 3.0, 4.0, 6.0, -0.0, -0.5, -1.0, -1.5, -2.0, -3.0, -4.0, -6.0])


def pack_weight(w, fmt):
    k, n = w.shape
    w = f64(np.asarray(w, np.float32).astype(ml_dtypes.bfloat16)).reshape(k // 32, 32, n)
    amax = np.abs(w).max(1)
    if fmt == "e4m3":
        byte = np.frexp(amax)[1] - 1 + 127 - 7
    else:
        mant, ex = np.frexp(amax / 6.0)
        byte = np.where(mant > 0.5, ex, ex - 1) + 127
    byte = np.clip(np.where(amax > 0, byte, 1), 1, 254)
    scaled = (w * np.exp2(127.0 - byte)[:, None, :]).reshape(k, n).astype(np.float32)
    by_word = np.ascontiguousarray(scaled.reshape(k // 512, 128, 4, n).transpose(0, 1, 3, 2))
    if fmt == "e4m3":
        words = by_word.astype(ml_dtypes.float8_e4m3fn).view(np.uint8)
    else:
        c = by_word.astype(ml_dtypes.float4_e2m1fn).view(np.uint8) & 0xF
        words = (c[..., 0::2] | (c[..., 1::2] << 4)).reshape(k // 512, 128, 2 * n)
    return np.ascontiguousarray(words), np.ascontiguousarray(byte.astype(np.uint8).reshape(k // 512, 16, n))


def unpack_weight(words, scales, fmt):
    g, _, n = scales.shape
    words = np.ascontiguousarray(words).reshape(g, 128, n, -1)
    if fmt == "e4m3":
        vals = words.view(ml_dtypes.float8_e4m3fn).astype(np.float64)
    else:
        nib = np.empty((g, 128, n, 4), np.uint8)
        nib[..., 0::2] = words & 0xF
        nib[..., 1::2] = words >> 4
        vals = E2M1[nib]
    vals = vals * np.repeat(np.exp2(scales.astype(np.float64) - 127.0), 8, axis=1)[..., None]
    return vals.transpose(0, 1, 3, 2).reshape(g * 512, n)


D, T, I, Q, J, U, G, M = 512, 2048, 512, 128, 512, 1024, 64, 512


def setup_inputs():
    n = np.random.standard_normal
    idx = np.random.permutation(T)[:I]
    idx2 = np.random.permutation(U)[:J]
    idx3 = np.random.permutation(M)[:G]
    fd = mx_kscale(D)
    fj = mx_kscale(J)
    tiesp = pack_weight(n((J, T)) * 0.08 / fj[:, None], "e2m1")
    return {
        "query": (n((D, Q)) * 0.65 / np.sqrt(D) * fd[:, None]).astype(np.float32),
        "hubs": (n((D, U)) / fd[:, None]).astype(np.float32),
        "hf": (np.random.uniform(0.5, 2.0, (J, 1)) * fj[:, None]).astype(np.float32),
        "ties_words": tiesp[0],
        "ties_scales": tiesp[1],
        "bar": (np.random.uniform(0.0, 0.8, (Q, 1))).astype(np.float32),
        "reserve": (np.random.uniform(20.0, 80.0, (Q, 1))).astype(np.float32),
        "worth": np.tile(np.random.uniform(0.2, 2.0, T), (128, 1)).astype(np.float32),
        "old": (1.0 * n((Q, M))).astype(np.float32),
        "offs": striped(idx),
        "offs2": striped(idx2),
        "offs3": striped(idx3),
    }


def reference(query, hubs, hf, ties_words, ties_scales, bar, reserve, worth, old, offs, offs2, offs3):
    idx = unstriped(offs)
    idx2 = unstriped(offs2)
    idx3 = unstriped(offs3)
    tiesu = unpack_weight(ties_words, ties_scales, "e2m1")
    hubsidx2q = mxq(f64(hubs)[:, idx2], 0, "e4m3")
    queryq = mxq(f64(query), 0, "e4m3")
    hb = hubsidx2q.T @ queryq
    hp = np.maximum(hb, 0.0) * f64(hf)
    hpq = mxq(hp, 0, "e4m3")
    tiesidxg = tiesu[:, idx]
    s = hpq.T @ tiesidxg
    ce = s - np.mean(s, axis=1, keepdims=True)
    sd = np.sqrt(np.mean(np.square(ce), axis=1, keepdims=True) + 0.1)
    p = np.square(np.maximum(ce / sd - f64(bar), 0.0))
    w = p / (np.sum(p, axis=1, keepdims=True) + f64(reserve))
    ws = w * f64(worth)[:1][:, idx] * 256.0
    wp = ws.reshape(Q, G, I // G).sum(axis=2)
    wf = np.zeros((Q, M))
    wf[:, idx3] = wp
    y = f64(old) + wf
    return y

@@ -1,0 +1,228 @@
+from contextlib import ExitStack
+
+import concourse.mybir as mybir
+
+F32 = mybir.dt.float32
+BF16 = mybir.dt.bfloat16
+I32 = mybir.dt.int32
+U32 = mybir.dt.uint32
+U16 = mybir.dt.uint16
+U8 = mybir.dt.uint8
+FP8X4 = mybir.dt.float8_e4m3fn_x4
+FP4X4 = mybir.dt.float4_e2m1fn_x4
+ALU = mybir.AluOpType
+ACT = mybir.ActivationFunctionType
+AXIS = mybir.AxisListType
+
+P = 128
+PACK = 4
+D, T, I, Q, J, U, G, M = 512, 2048, 512, 128, 512, 1024, 64, 512
+RUN = I // G
+HALF = I // 2
+PER_COL = 16
+S_VEC = 64
+S_ACT = P - S_VEC
+
+FLOPS = 2 * J * D * Q + 2 * Q * J * I
+
+
+def tile_attend_relayed_outliers_pagesums_kernel(
+    tc, query, hubs, hf, ties_words, ties_scales, bar, reserve, worth, old, offs, offs2, offs3, out
+):
+    nc = tc.nc
+    with ExitStack() as ctx:
+        keep = ctx.enter_context(tc.tile_pool(name="keep", bufs=1))
+        psum = ctx.enter_context(tc.psum_pool(name="psum", bufs=1))
+
+        token_list = keep.tile([P, I // PER_COL], U16, name="token_list")
+        hub_list = keep.tile([P, J // PER_COL], U16, name="hub_list")
+        column_list = keep.tile([P, G // PER_COL], U16, name="column_list")
+
+        scale_pool = keep.tile([P, T], U8, name="scale_pool", align_bytes=64)
+        nc.vector.memset(scale_pool[:].bitcast(I32), 0)
+        tie_scales = keep.tile([P, I], U8, name="tie_scales", align_bytes=64)
+        nc.gpsimd.memset(tie_scales[:].bitcast(I32), 0)
+        placed = keep.tile([P, M], F32, name="placed")
+        nc.gpsimd.memset(placed[:], 0.0)
+
+        hf_t = keep.tile([P, PACK], F32, name="hf_t")
+        bar_t = keep.tile([P, 1], F32, name="bar_t")
+        reserve_t = keep.tile([P, 1], F32, name="reserve_t")
+        nc.gpsimd.dma_start(hf_t[:], hf.rearrange("(p r) o -> p (r o)", r=PACK))
+        nc.gpsimd.dma_start(bar_t[:], bar)
+        nc.gpsimd.dma_start(reserve_t[:], reserve)
+
+        query_raw = keep.tile([P, PACK, Q], F32, name="query_raw")
+        nc.sync.dma_start(token_list[:], offs)
+        nc.sync.dma_start(query_raw[:], query.rearrange("(p t) q -> p t q", t=PACK))
+        nc.sync.dma_start(hub_list[:], offs2)
+        nc.sync.dma_start(scale_pool[0:P:8, :].bitcast(I32), ties_scales[0].bitcast(I32))
+        hub_rows = hubs.rearrange("(p t) u -> t p u", t=PACK)
+        hub_pool = [keep.tile([P, U], F32, name=f"hub_pool{t}") for t in range(PACK)]
+        for t in range(PACK):
+            nc.sync.dma_start(hub_pool[t][:], hub_rows[t])
+
+        scale_rows = keep.tile([P, I], U8, name="scale_rows", align_bytes=64)
+        nc.vector.tensor_copy(scale_rows[:], scale_pool[:].indirect(token_list[:]))
+        for quad in range(4):
+            nc.sync.dma_start(
+                tie_scales[32 * quad : 32 * quad + 4, :].bitcast(I32),
+                scale_rows[32 * quad : 32 * quad + 32 : 8, :].bitcast(I32),
+            )
+
+        word_pool = keep.tile([P, T], U16, name="word_pool", align_bytes=64)
+        nc.sync.dma_start(word_pool[:].bitcast(I32), ties_words[0].bitcast(I32))
+        worth_pool = keep.tile([P, T], F32, name="worth_pool")
+        nc.sync.dma_start(worth_pool[:], worth)
+        nc.sync.dma_start(column_list[:], offs3)
+        old_t = keep.tile([P, M], F32, name="old_t")
+        nc.sync.dma_start(old_t[:], old)
+
+        query_bf = keep.tile([P, Q, PACK], BF16, name="query_bf", align_bytes=64)
+        nc.scalar.copy(query_bf[:], query_raw[:].rearrange("p t q -> p q t"))
+        query_codes = keep.tile([P, Q], U32, name="query_codes", align_bytes=64)
+        query_scales = keep.tile([P, Q], U8, name="query_scales", align_bytes=64)
+        nc.vector.quantize_mx(
+            out=query_codes[:].bitcast(FP8X4), scales=query_scales[:], in_=query_bf[:].rearrange("p q t -> p (q t)")
+        )
+
+        neg_bar = keep.tile([P, 1], F32, name="neg_bar")
+        nc.gpsimd.tensor_scalar(neg_bar[:], bar_t[:], -1.0, 0.0, ALU.mult, ALU.add)
+        reserve_part = keep.tile([P, 1], F32, name="reserve_part")
+        nc.gpsimd.tensor_scalar(reserve_part[:], reserve_t[:], 1.0 / 256.0, 0.0, ALU.mult, ALU.add)
+
+        hub_bf = keep.tile([P, PACK, P, PACK], BF16, name="hub_bf", tag="first", align_bytes=64)
+        split = S_VEC * PACK // PER_COL
+        for pair in range(2):
+            staged = keep.tile([P, 2, S_ACT * PACK], BF16, name=f"staged{pair}")
+            for e in range(2):
+                t = 2 * pair + e
+                nc.vector.tensor_copy(
+                    hub_bf[:, :, 0:S_VEC, t].rearrange("p r s -> p s r"),
+                    hub_pool[t][:].indirect(hub_list[:, 0:split]),
+                )
+                nc.scalar.activation(staged[:, e, :], hub_pool[t][:].indirect(hub_list[:, split:]), ACT.Copy)
+            nc.vector.tensor_copy(
+                hub_bf[:, :, S_VEC:, 2 * pair : 2 * pair + 2],
+                staged[:].rearrange("p e (s r) -> p r s e", r=PACK),
+            )
+
+        hub_codes = keep.tile([P, J], U32, name="hub_codes", align_bytes=64)
+        hub_scales = keep.tile([P, J], U8, name="hub_scales", align_bytes=64)
+        hb = psum.tile([P, PACK, Q], F32, name="hb")
+        for r in range(PACK):
+            cols = slice(r * P, (r + 1) * P)
+            nc.vector.quantize_mx(
+                out=hub_codes[:, cols].bitcast(FP8X4),
+                scales=hub_scales[:, cols],
+                in_=hub_bf[:, r].rearrange("p s t -> p (s t)"),
+            )
+            nc.tensor.matmul_mx(
+                out=hb[:, r, :],
+                lhsT=hub_codes[:, cols].bitcast(FP8X4),
+                lhsT_scale=hub_scales[:, cols],
+                rhs=query_codes[:].bitcast(FP8X4),
+                rhs_scale=query_scales[:],
+                start=True,
+                stop=True,
+            )
+
+        list_half = HALF // PER_COL
+        words_a = keep.tile([P, HALF], U16, name="words_a", tag="first", align_bytes=64)
+        nc.vector.tensor_copy(words_a[:], word_pool[:].indirect(token_list[:, 0:list_half]))
+
+        hp_bf = keep.tile([P, Q, PACK], BF16, name="hp_bf", tag="second", align_bytes=64)
+        row_halves = [slice(0, Q // 2), slice(Q // 2, Q)]
+        for rows in row_halves:
+            nc.vector.scalar_tensor_tensor(
+                hp_bf[:, rows, :],
+                hb[:, :, rows].rearrange("p r q -> p q r"),
+                0.0,
+                hf_t[:].unsqueeze(1).broadcast_to([P, Q // 2, PACK]),
+                ALU.max,
+                ALU.mult,
+            )
+        hp_codes = keep.tile([P, Q], U32, name="hp_codes", align_bytes=64)
+        hp_scales = keep.tile([P, Q], U8, name="hp_scales", align_bytes=64)
+        for rows in row_halves:
+            nc.vector.quantize_mx(
+                out=hp_codes[:, rows].bitcast(FP8X4),
+                scales=hp_scales[:, rows],
+                in_=hp_bf[:, rows, :].rearrange("p q r -> p (q r)"),
+            )
+        words_b = keep.tile([P, HALF], U16, name="words_b", tag="second", align_bytes=64)
+        nc.vector.tensor_copy(words_b[:], word_pool[:].indirect(token_list[:, list_half:]))
+
+        worth_g = keep.tile([P, I], F32, name="worth_g")
+        halves = [slice(0, HALF), slice(HALF, I)]
+        for h in range(2):
+            nc.scalar.activation(
+                worth_g[:, halves[h]],
+                worth_pool[:].indirect(token_list[:, h * list_half : (h + 1) * list_half]),
+                ACT.Copy,
+            )
+
+        score = [psum.tile([P, HALF], F32, name=f"score{h}") for h in range(2)]
+        stats = keep.tile([P, 2, 6], F32, name="stats")
+        for h, words in enumerate((words_a, words_b)):
+            nc.tensor.matmul_mx(
+                out=score[h][:],
+                lhsT=hp_codes[:].bitcast(FP8X4),
+                lhsT_scale=hp_scales[:],
+                rhs=words[:].bitcast(FP4X4),
+                rhs_scale=tie_scales[:, halves[h]],
+                start=True,
+                stop=True,
+            )
+            nc.vector.bn_stats(stats[:, h, :], score[h][:])
+        mean_var = keep.tile([P, 2], F32, name="mean_var")
+        nc.vector.bn_aggr(mean_var[:], stats[:].rearrange("p h s -> p (h s)"))
+
+        sd = keep.tile([P, 1], F32, name="sd")
+        nc.scalar.activation(sd[:], mean_var[:, 1:2], ACT.Sqrt, bias=0.1)
+        neg_mean = keep.tile([P, 1], F32, name="neg_mean")
+        nc.vector.tensor_scalar(neg_mean[:], mean_var[:, 0:1], -1.0, None, ALU.mult)
+        floor = keep.tile([P, 1], F32, name="floor")
+        nc.vector.tensor_scalar(floor[:], mean_var[:, 1:2], 0.1, reserve_part[:], ALU.add, ALU.mult)
+        neg_level = keep.tile([P, 1], F32, name="neg_level")
+        nc.scalar.activation(neg_level[:], sd[:], ACT.Identity, bias=neg_mean[:], scale=neg_bar[:])
+
+        excess = keep.tile([P, I], F32, name="excess")
+        priced = keep.tile([P, I], F32, name="priced")
+        for h in range(2):
+            nc.scalar.activation(excess[:, halves[h]], score[h][:], ACT.Relu, bias=neg_level[:])
+            nc.vector.scalar_tensor_tensor(
+                priced[:, halves[1 - h]],
+                score[1 - h][:],
+                neg_level[:],
+                worth_g[:, halves[1 - h]],
+                ALU.add,
+                ALU.mult,
+            )
+        squares = keep.tile([P, I], F32, name="squares")
+        total = keep.tile([P, 1], F32, name="total")
+        nc.scalar.activation(squares[:], excess[:], ACT.Square, accum_out=total[:])
+        denom = keep.tile([P, 1], F32, name="denom")
+        nc.scalar.activation(denom[:], total[:], ACT.Identity, bias=floor[:], scale=1.0 / 256.0)
+
+        weighted = keep.tile([P, I], F32, name="weighted")
+        sums = keep.tile([P, G], F32, name="sums")
+        for h in (1, 0):
+            nc.vector.tensor_tensor(weighted[:, halves[h]], excess[:, halves[h]], priced[:, halves[h]], ALU.mult)
+        for h in (1, 0):
+            nc.vector.tensor_reduce(
+                sums[:, h * G // 2 : (h + 1) * G // 2],
+                weighted[:, halves[h]].rearrange("p (g e) -> p g e", e=RUN),
+                AXIS.X,
+                ALU.add,
+            )
+        inverse = keep.tile([P, 1], F32, name="inverse")
+        nc.vector.reciprocal(inverse[:], denom[:])
+        nc.vector.tensor_copy(placed[:].indirect(column_list[:]), sums[:])
+
+        result = keep.tile([P, M], F32, name="result")
+        for h, queue in enumerate((nc.sync, nc.scalar)):
+            nc.vector.scalar_tensor_tensor(
+                result[:, halves[h]], placed[:, halves[h]], inverse[:], old_t[:, halves[h]], ALU.mult, ALU.add
+            )
+            queue.dma_start(out[:, halves[h]], result[:, halves[h]])

@@ -20,8 +20,7 @@ D, T, I, Q, J, U, G, M = 512, 2048, 512, 128, 512, 1024, 64, 512
 RUN = I // G
 HALF = I // 2
 PER_COL = 16
-S_VEC = 64
-S_ACT = P - S_VEC
+S_VEC = (40, 72)
 
 FLOPS = 2 * J * D * Q + 2 * Q * J * I
 
@@ -45,6 +44,11 @@ def tile_attend_relayed_outliers_pagesums_kernel(
         placed = keep.tile([P, M], F32, name="placed")
         nc.gpsimd.memset(placed[:], 0.0)
 
+        warm_in = keep.tile([P, 1], F32, name="warm_in")
+        nc.gpsimd.memset(warm_in[:], 1.0)
+        warm_out = keep.tile([P, 1], F32, name="warm_out")
+        nc.scalar.activation(warm_out[:], warm_in[:], ACT.Sqrt)
+
         hf_t = keep.tile([P, PACK], F32, name="hf_t")
         bar_t = keep.tile([P, 1], F32, name="bar_t")
         reserve_t = keep.tile([P, 1], F32, name="reserve_t")
@@ -54,13 +58,15 @@ def tile_attend_relayed_outliers_pagesums_kernel(
 
         query_raw = keep.tile([P, PACK, Q], F32, name="query_raw")
         nc.sync.dma_start(token_list[:], offs)
-        nc.sync.dma_start(query_raw[:], query.rearrange("(p t) q -> p t q", t=PACK))
-        nc.sync.dma_start(hub_list[:], offs2)
         nc.sync.dma_start(scale_pool[0:P:8, :].bitcast(I32), ties_scales[0].bitcast(I32))
+        nc.sync.dma_start(hub_list[:], offs2)
         hub_rows = hubs.rearrange("(p t) u -> t p u", t=PACK)
         hub_pool = [keep.tile([P, U], F32, name=f"hub_pool{t}") for t in range(PACK)]
         for t in range(PACK):
-            nc.sync.dma_start(hub_pool[t][:], hub_rows[t])
+            (nc.scalar if t == 0 else nc.sync).dma_start(hub_pool[t][:], hub_rows[t])
+        nc.sync.dma_start(query_raw[:], query.rearrange("(p t) q -> p t q", t=PACK))
+        word_pool = keep.tile([P, T], U16, name="word_pool", align_bytes=64)
+        nc.sync.dma_start(word_pool[:].bitcast(I32), ties_words[0].bitcast(I32))
 
         scale_rows = keep.tile([P, I], U8, name="scale_rows", align_bytes=64)
         nc.vector.tensor_copy(scale_rows[:], scale_pool[:].indirect(token_list[:]))
@@ -70,41 +76,40 @@ def tile_attend_relayed_outliers_pagesums_kernel(
                 scale_rows[32 * quad : 32 * quad + 32 : 8, :].bitcast(I32),
             )
 
-        word_pool = keep.tile([P, T], U16, name="word_pool", align_bytes=64)
-        nc.sync.dma_start(word_pool[:].bitcast(I32), ties_words[0].bitcast(I32))
-        worth_pool = keep.tile([P, T], F32, name="worth_pool")
+        worth_pool = keep.tile([P, T], F32, name="worth_pool", tag="third")
         nc.sync.dma_start(worth_pool[:], worth)
         nc.sync.dma_start(column_list[:], offs3)
         old_t = keep.tile([P, M], F32, name="old_t")
         nc.sync.dma_start(old_t[:], old)
 
-        query_bf = keep.tile([P, Q, PACK], BF16, name="query_bf", align_bytes=64)
-        nc.scalar.copy(query_bf[:], query_raw[:].rearrange("p t q -> p q t"))
-        query_codes = keep.tile([P, Q], U32, name="query_codes", align_bytes=64)
-        query_scales = keep.tile([P, Q], U8, name="query_scales", align_bytes=64)
-        nc.vector.quantize_mx(
-            out=query_codes[:].bitcast(FP8X4), scales=query_scales[:], in_=query_bf[:].rearrange("p q t -> p (q t)")
-        )
-
-        neg_bar = keep.tile([P, 1], F32, name="neg_bar")
-        nc.gpsimd.tensor_scalar(neg_bar[:], bar_t[:], -1.0, 0.0, ALU.mult, ALU.add)
-        reserve_part = keep.tile([P, 1], F32, name="reserve_part")
-        nc.gpsimd.tensor_scalar(reserve_part[:], reserve_t[:], 1.0 / 256.0, 0.0, ALU.mult, ALU.add)
-
         hub_bf = keep.tile([P, PACK, P, PACK], BF16, name="hub_bf", tag="first", align_bytes=64)
-        split = S_VEC * PACK // PER_COL
-        for pair in range(2):
-            staged = keep.tile([P, 2, S_ACT * PACK], BF16, name=f"staged{pair}")
+        for pair, s_vec in enumerate(S_VEC):
+            split = s_vec * PACK // PER_COL
+            staged = keep.tile([P, 2, (P - s_vec) * PACK], BF16, name=f"staged{pair}")
             for e in range(2):
                 t = 2 * pair + e
                 nc.vector.tensor_copy(
-                    hub_bf[:, :, 0:S_VEC, t].rearrange("p r s -> p s r"),
+                    hub_bf[:, :, 0:s_vec, t].rearrange("p r s -> p s r"),
                     hub_pool[t][:].indirect(hub_list[:, 0:split]),
                 )
                 nc.scalar.activation(staged[:, e, :], hub_pool[t][:].indirect(hub_list[:, split:]), ACT.Copy)
-            nc.vector.tensor_copy(
-                hub_bf[:, :, S_VEC:, 2 * pair : 2 * pair + 2],
-                staged[:].rearrange("p e (s r) -> p r s e", r=PACK),
+            for r0 in (0, 2):
+                nc.vector.tensor_copy(
+                    hub_bf[:, r0 : r0 + 2, s_vec:, 2 * pair : 2 * pair + 2],
+                    staged[:].rearrange("p e (s r) -> p r s e", r=PACK)[:, r0 : r0 + 2],
+                )
+
+        query_bf = keep.tile([P, Q, PACK], BF16, name="query_bf", align_bytes=64)
+        row_halves = [slice(0, Q // 2), slice(Q // 2, Q)]
+        for rows in row_halves:
+            nc.scalar.copy(query_bf[:, rows, :], query_raw[:, :, rows].rearrange("p t q -> p q t"))
+        query_codes = keep.tile([P, Q], U32, name="query_codes", align_bytes=64)
+        query_scales = keep.tile([P, Q], U8, name="query_scales", align_bytes=64)
+        for rows in row_halves:
+            nc.vector.quantize_mx(
+                out=query_codes[:, rows].bitcast(FP8X4),
+                scales=query_scales[:, rows],
+                in_=query_bf[:, rows, :].rearrange("p q t -> p (q t)"),
             )
 
         hub_codes = keep.tile([P, J], U32, name="hub_codes", align_bytes=64)
@@ -132,7 +137,6 @@ def tile_attend_relayed_outliers_pagesums_kernel(
         nc.vector.tensor_copy(words_a[:], word_pool[:].indirect(token_list[:, 0:list_half]))
 
         hp_bf = keep.tile([P, Q, PACK], BF16, name="hp_bf", tag="second", align_bytes=64)
-        row_halves = [slice(0, Q // 2), slice(Q // 2, Q)]
         for rows in row_halves:
             nc.vector.scalar_tensor_tensor(
                 hp_bf[:, rows, :],
@@ -160,9 +164,14 @@ def tile_attend_relayed_outliers_pagesums_kernel(
                 worth_g[:, halves[h]],
                 worth_pool[:].indirect(token_list[:, h * list_half : (h + 1) * list_half]),
                 ACT.Copy,
+                scale=256.0,
             )
 
+        neg_bar = keep.tile([P, 1], F32, name="neg_bar")
+        nc.gpsimd.tensor_scalar(neg_bar[:], bar_t[:], -1.0, 0.0, ALU.mult, ALU.add)
         score = [psum.tile([P, HALF], F32, name=f"score{h}") for h in range(2)]
+        late = keep.tile([P, I + 1], F32, name="late", tag="third")
+        score_sb = late[:, 0:I]
         stats = keep.tile([P, 2, 6], F32, name="stats")
         for h, words in enumerate((words_a, words_b)):
             nc.tensor.matmul_mx(
@@ -175,27 +184,28 @@ def tile_attend_relayed_outliers_pagesums_kernel(
                 stop=True,
             )
             nc.vector.bn_stats(stats[:, h, :], score[h][:])
+            nc.scalar.copy(score_sb[:, halves[h]], score[h][:])
         mean_var = keep.tile([P, 2], F32, name="mean_var")
         nc.vector.bn_aggr(mean_var[:], stats[:].rearrange("p h s -> p (h s)"))
 
-        sd = keep.tile([P, 1], F32, name="sd")
-        nc.scalar.activation(sd[:], mean_var[:, 1:2], ACT.Sqrt, bias=0.1)
+        sd = late[:, I : I + 1]
+        nc.scalar.activation(sd, mean_var[:, 1:2], ACT.Sqrt, bias=0.1)
         neg_mean = keep.tile([P, 1], F32, name="neg_mean")
         nc.vector.tensor_scalar(neg_mean[:], mean_var[:, 0:1], -1.0, None, ALU.mult)
         floor = keep.tile([P, 1], F32, name="floor")
-        nc.vector.tensor_scalar(floor[:], mean_var[:, 1:2], 0.1, reserve_part[:], ALU.add, ALU.mult)
+        nc.vector.tensor_scalar(floor[:], mean_var[:, 1:2], 0.1, reserve_t[:], ALU.add, ALU.mult)
         neg_level = keep.tile([P, 1], F32, name="neg_level")
-        nc.scalar.activation(neg_level[:], sd[:], ACT.Identity, bias=neg_mean[:], scale=neg_bar[:])
+        nc.scalar.activation(neg_level[:], sd, ACT.Identity, bias=neg_mean[:], scale=neg_bar[:])
 
         excess = keep.tile([P, I], F32, name="excess")
         priced = keep.tile([P, I], F32, name="priced")
         for h in range(2):
-            nc.scalar.activation(excess[:, halves[h]], score[h][:], ACT.Relu, bias=neg_level[:])
+            nc.scalar.activation(excess[:, halves[h]], score_sb[:, halves[h]], ACT.Relu, bias=neg_level[:])
             nc.vector.scalar_tensor_tensor(
-                priced[:, halves[1 - h]],
-                score[1 - h][:],
+                priced[:, halves[h]],
+                score[h][:],
                 neg_level[:],
-                worth_g[:, halves[1 - h]],
+                worth_g[:, halves[h]],
                 ALU.add,
                 ALU.mult,
             )
@@ -203,13 +213,13 @@ def tile_attend_relayed_outliers_pagesums_kernel(
         total = keep.tile([P, 1], F32, name="total")
         nc.scalar.activation(squares[:], excess[:], ACT.Square, accum_out=total[:])
         denom = keep.tile([P, 1], F32, name="denom")
-        nc.scalar.activation(denom[:], total[:], ACT.Identity, bias=floor[:], scale=1.0 / 256.0)
+        nc.scalar.activation(denom[:], total[:], ACT.Identity, bias=floor[:])
 
         weighted = keep.tile([P, I], F32, name="weighted")
         sums = keep.tile([P, G], F32, name="sums")
-        for h in (1, 0):
+        for h in range(2):
             nc.vector.tensor_tensor(weighted[:, halves[h]], excess[:, halves[h]], priced[:, halves[h]], ALU.mult)
-        for h in (1, 0):
+        for h in range(2):
             nc.vector.tensor_reduce(
                 sums[:, h * G // 2 : (h + 1) * G // 2],
                 weighted[:, halves[h]].rearrange("p (g e) -> p g e", e=RUN),

@@ -20,7 +20,7 @@ D, T, I, Q, J, U, G, M = 512, 2048, 512, 128, 512, 1024, 64, 512
 RUN = I // G
 HALF = I // 2
 PER_COL = 16
-S_VEC = (40, 72)
+S_VEC = (48, 56)
 
 FLOPS = 2 * J * D * Q + 2 * Q * J * I
 

from contextlib import ExitStack

import concourse.mybir as mybir

F32 = mybir.dt.float32
BF16 = mybir.dt.bfloat16
I32 = mybir.dt.int32
U32 = mybir.dt.uint32
U16 = mybir.dt.uint16
U8 = mybir.dt.uint8
FP8X4 = mybir.dt.float8_e4m3fn_x4
FP4X4 = mybir.dt.float4_e2m1fn_x4
ALU = mybir.AluOpType
ACT = mybir.ActivationFunctionType
AXIS = mybir.AxisListType

P = 128
PACK = 4
D, T, I, Q, J, U, G, M = 512, 2048, 512, 128, 512, 1024, 64, 512
RUN = I // G
HALF = I // 2
PER_COL = 16
S_VEC = (48, 56)

FLOPS = 2 * J * D * Q + 2 * Q * J * I


def tile_attend_relayed_outliers_pagesums_kernel(
    tc, query, hubs, hf, ties_words, ties_scales, bar, reserve, worth, old, offs, offs2, offs3, out
):
    nc = tc.nc
    with ExitStack() as ctx:
        keep = ctx.enter_context(tc.tile_pool(name="keep", bufs=1))
        psum = ctx.enter_context(tc.psum_pool(name="psum", bufs=1))

        token_list = keep.tile([P, I // PER_COL], U16, name="token_list")
        hub_list = keep.tile([P, J // PER_COL], U16, name="hub_list")
        column_list = keep.tile([P, G // PER_COL], U16, name="column_list")

        scale_pool = keep.tile([P, T], U8, name="scale_pool", align_bytes=64)
        nc.vector.memset(scale_pool[:].bitcast(I32), 0)
        tie_scales = keep.tile([P, I], U8, name="tie_scales", align_bytes=64)
        nc.gpsimd.memset(tie_scales[:].bitcast(I32), 0)
        placed = keep.tile([P, M], F32, name="placed")
        nc.gpsimd.memset(placed[:], 0.0)

        warm_in = keep.tile([P, 1], F32, name="warm_in")
        nc.gpsimd.memset(warm_in[:], 1.0)
        warm_out = keep.tile([P, 1], F32, name="warm_out")
        nc.scalar.activation(warm_out[:], warm_in[:], ACT.Sqrt)

        hf_t = keep.tile([P, PACK], F32, name="hf_t")
        bar_t = keep.tile([P, 1], F32, name="bar_t")
        reserve_t = keep.tile([P, 1], F32, name="reserve_t")
        nc.gpsimd.dma_start(hf_t[:], hf.rearrange("(p r) o -> p (r o)", r=PACK))
        nc.gpsimd.dma_start(bar_t[:], bar)
        nc.gpsimd.dma_start(reserve_t[:], reserve)

        query_raw = keep.tile([P, PACK, Q], F32, name="query_raw")
        nc.sync.dma_start(token_list[:], offs)
        nc.sync.dma_start(scale_pool[0:P:8, :].bitcast(I32), ties_scales[0].bitcast(I32))
        nc.sync.dma_start(hub_list[:], offs2)
        hub_rows = hubs.rearrange("(p t) u -> t p u", t=PACK)
        hub_pool = [keep.tile([P, U], F32, name=f"hub_pool{t}") for t in range(PACK)]
        for t in range(PACK):
            (nc.scalar if t == 0 else nc.sync).dma_start(hub_pool[t][:], hub_rows[t])
        nc.sync.dma_start(query_raw[:], query.rearrange("(p t) q -> p t q", t=PACK))
        word_pool = keep.tile([P, T], U16, name="word_pool", align_bytes=64)
        nc.sync.dma_start(word_pool[:].bitcast(I32), ties_words[0].bitcast(I32))

        scale_rows = keep.tile([P, I], U8, name="scale_rows", align_bytes=64)
        nc.vector.tensor_copy(scale_rows[:], scale_pool[:].indirect(token_list[:]))
        for quad in range(4):
            nc.sync.dma_start(
                tie_scales[32 * quad : 32 * quad + 4, :].bitcast(I32),
                scale_rows[32 * quad : 32 * quad + 32 : 8, :].bitcast(I32),
            )

        worth_pool = keep.tile([P, T], F32, name="worth_pool", tag="third")
        nc.sync.dma_start(worth_pool[:], worth)
        nc.sync.dma_start(column_list[:], offs3)
        old_t = keep.tile([P, M], F32, name="old_t")
        nc.sync.dma_start(old_t[:], old)

        hub_bf = keep.tile([P, PACK, P, PACK], BF16, name="hub_bf", tag="first", align_bytes=64)
        for pair, s_vec in enumerate(S_VEC):
            split = s_vec * PACK // PER_COL
            staged = keep.tile([P, 2, (P - s_vec) * PACK], BF16, name=f"staged{pair}")
            for e in range(2):
                t = 2 * pair + e
                nc.vector.tensor_copy(
                    hub_bf[:, :, 0:s_vec, t].rearrange("p r s -> p s r"),
                    hub_pool[t][:].indirect(hub_list[:, 0:split]),
                )
                nc.scalar.activation(staged[:, e, :], hub_pool[t][:].indirect(hub_list[:, split:]), ACT.Copy)
            for r0 in (0, 2):
                nc.vector.tensor_copy(
                    hub_bf[:, r0 : r0 + 2, s_vec:, 2 * pair : 2 * pair + 2],
                    staged[:].rearrange("p e (s r) -> p r s e", r=PACK)[:, r0 : r0 + 2],
                )

        query_bf = keep.tile([P, Q, PACK], BF16, name="query_bf", align_bytes=64)
        row_halves = [slice(0, Q // 2), slice(Q // 2, Q)]
        for rows in row_halves:
            nc.scalar.copy(query_bf[:, rows, :], query_raw[:, :, rows].rearrange("p t q -> p q t"))
        query_codes = keep.tile([P, Q], U32, name="query_codes", align_bytes=64)
        query_scales = keep.tile([P, Q], U8, name="query_scales", align_bytes=64)
        for rows in row_halves:
            nc.vector.quantize_mx(
                out=query_codes[:, rows].bitcast(FP8X4),
                scales=query_scales[:, rows],
                in_=query_bf[:, rows, :].rearrange("p q t -> p (q t)"),
            )

        hub_codes = keep.tile([P, J], U32, name="hub_codes", align_bytes=64)
        hub_scales = keep.tile([P, J], U8, name="hub_scales", align_bytes=64)
        hb = psum.tile([P, PACK, Q], F32, name="hb")
        for r in range(PACK):
            cols = slice(r * P, (r + 1) * P)
            nc.vector.quantize_mx(
                out=hub_codes[:, cols].bitcast(FP8X4),
                scales=hub_scales[:, cols],
                in_=hub_bf[:, r].rearrange("p s t -> p (s t)"),
            )
            nc.tensor.matmul_mx(
                out=hb[:, r, :],
                lhsT=hub_codes[:, cols].bitcast(FP8X4),
                lhsT_scale=hub_scales[:, cols],
                rhs=query_codes[:].bitcast(FP8X4),
                rhs_scale=query_scales[:],
                start=True,
                stop=True,
            )

        list_half = HALF // PER_COL
        words_a = keep.tile([P, HALF], U16, name="words_a", tag="first", align_bytes=64)
        nc.vector.tensor_copy(words_a[:], word_pool[:].indirect(token_list[:, 0:list_half]))

        hp_bf = keep.tile([P, Q, PACK], BF16, name="hp_bf", tag="second", align_bytes=64)
        for rows in row_halves:
            nc.vector.scalar_tensor_tensor(
                hp_bf[:, rows, :],
                hb[:, :, rows].rearrange("p r q -> p q r"),
                0.0,
                hf_t[:].unsqueeze(1).broadcast_to([P, Q // 2, PACK]),
                ALU.max,
                ALU.mult,
            )
        hp_codes = keep.tile([P, Q], U32, name="hp_codes", align_bytes=64)
        hp_scales = keep.tile([P, Q], U8, name="hp_scales", align_bytes=64)
        for rows in row_halves:
            nc.vector.quantize_mx(
                out=hp_codes[:, rows].bitcast(FP8X4),
                scales=hp_scales[:, rows],
                in_=hp_bf[:, rows, :].rearrange("p q r -> p (q r)"),
            )
        words_b = keep.tile([P, HALF], U16, name="words_b", tag="second", align_bytes=64)
        nc.vector.tensor_copy(words_b[:], word_pool[:].indirect(token_list[:, list_half:]))

        worth_g = keep.tile([P, I], F32, name="worth_g")
        halves = [slice(0, HALF), slice(HALF, I)]
        for h in range(2):
            nc.scalar.activation(
                worth_g[:, halves[h]],
                worth_pool[:].indirect(token_list[:, h * list_half : (h + 1) * list_half]),
                ACT.Copy,
                scale=256.0,
            )

        neg_bar = keep.tile([P, 1], F32, name="neg_bar")
        nc.gpsimd.tensor_scalar(neg_bar[:], bar_t[:], -1.0, 0.0, ALU.mult, ALU.add)
        score = [psum.tile([P, HALF], F32, name=f"score{h}") for h in range(2)]
        late = keep.tile([P, I + 1], F32, name="late", tag="third")
        score_sb = late[:, 0:I]
        stats = keep.tile([P, 2, 6], F32, name="stats")
        for h, words in enumerate((words_a, words_b)):
            nc.tensor.matmul_mx(
                out=score[h][:],
                lhsT=hp_codes[:].bitcast(FP8X4),
                lhsT_scale=hp_scales[:],
                rhs=words[:].bitcast(FP4X4),
                rhs_scale=tie_scales[:, halves[h]],
                start=True,
                stop=True,
            )
            nc.vector.bn_stats(stats[:, h, :], score[h][:])
            nc.scalar.copy(score_sb[:, halves[h]], score[h][:])
        mean_var = keep.tile([P, 2], F32, name="mean_var")
        nc.vector.bn_aggr(mean_var[:], stats[:].rearrange("p h s -> p (h s)"))

        sd = late[:, I : I + 1]
        nc.scalar.activation(sd, mean_var[:, 1:2], ACT.Sqrt, bias=0.1)
        neg_mean = keep.tile([P, 1], F32, name="neg_mean")
        nc.vector.tensor_scalar(neg_mean[:], mean_var[:, 0:1], -1.0, None, ALU.mult)
        floor = keep.tile([P, 1], F32, name="floor")
        nc.vector.tensor_scalar(floor[:], mean_var[:, 1:2], 0.1, reserve_t[:], ALU.add, ALU.mult)
        neg_level = keep.tile([P, 1], F32, name="neg_level")
        nc.scalar.activation(neg_level[:], sd, ACT.Identity, bias=neg_mean[:], scale=neg_bar[:])

        excess = keep.tile([P, I], F32, name="excess")
        priced = keep.tile([P, I], F32, name="priced")
        for h in range(2):
            nc.scalar.activation(excess[:, halves[h]], score_sb[:, halves[h]], ACT.Relu, bias=neg_level[:])
            nc.vector.scalar_tensor_tensor(
                priced[:, halves[h]],
                score[h][:],
                neg_level[:],
                worth_g[:, halves[h]],
                ALU.add,
                ALU.mult,
            )
        squares = keep.tile([P, I], F32, name="squares")
        total = keep.tile([P, 1], F32, name="total")
        nc.scalar.activation(squares[:], excess[:], ACT.Square, accum_out=total[:])
        denom = keep.tile([P, 1], F32, name="denom")
        nc.scalar.activation(denom[:], total[:], ACT.Identity, bias=floor[:])

        weighted = keep.tile([P, I], F32, name="weighted")
        sums = keep.tile([P, G], F32, name="sums")
        for h in range(2):
            nc.vector.tensor_tensor(weighted[:, halves[h]], excess[:, halves[h]], priced[:, halves[h]], ALU.mult)
        for h in range(2):
            nc.vector.tensor_reduce(
                sums[:, h * G // 2 : (h + 1) * G // 2],
                weighted[:, halves[h]].rearrange("p (g e) -> p g e", e=RUN),
                AXIS.X,
                ALU.add,
            )
        inverse = keep.tile([P, 1], F32, name="inverse")
        nc.vector.reciprocal(inverse[:], denom[:])
        nc.vector.tensor_copy(placed[:].indirect(column_list[:]), sums[:])

        result = keep.tile([P, M], F32, name="result")
        for h, queue in enumerate((nc.sync, nc.scalar)):
            nc.vector.scalar_tensor_tensor(
                result[:, halves[h]], placed[:, halves[h]], inverse[:], old_t[:, halves[h]], ALU.mult, ALU.add
            )
            queue.dma_start(out[:, halves[h]], result[:, halves[h]])
